import numpy as np
import ml_dtypes


def mxq(x, axis, fmt="e4m3"):
    dtype, down = {"e4m3": (ml_dtypes.float8_e4m3fn, 7), "e5m2": (ml_dtypes.float8_e5m2, 14)}[fmt]
    v = np.moveaxis(np.asarray(x, np.float32).astype(ml_dtypes.bfloat16).astype(np.float64), axis, -1)
    blocks = v.reshape(v.shape[:-1] + (-1, 32))
    amax = np.abs(blocks).max(-1, keepdims=True)
    byte = np.maximum(np.where(amax > 0, np.frexp(amax)[1] - 1 + 127, 0) - down, 1)
    scale = np.exp2(byte - 127.0)
    codes = (blocks / scale).astype(np.float32).astype(dtype).astype(np.float64)
    return np.moveaxis((codes * scale).reshape(v.shape), -1, axis)


WIDE = False


def mx_kscale(k):
    if not WIDE:
        return np.ones(k)
    levels = np.array([10, -10, 5, -5, 0])
    if k % 512:
        return np.exp2(np.random.permutation(np.resize(levels, k // 32))).repeat(32)
    a = np.empty((k // 512, 16))
    for p in range(k // 512):
        a[p, :8] = np.random.permutation(np.resize(levels, 8))
        for g in range(8):
            far = levels[np.abs(levels - a[p, g]) >= 10]
            a[p, g + 8] = far[np.random.randint(len(far))]
    return np.exp2(a.ravel()).repeat(32)


def f64(x):
    return np.asarray(x).astype(np.float64)


def striped(idx):
    return np.tile(idx.reshape(-1, 16).T, (8, 1)).astype(np.uint16)


def unstriped(offs):
    return offs[:16].T.reshape(-1).astype(np.int64)


E2M1 = np.array([0.0, 0.5, 1.0, 1.5, 2.0, 3.0, 4.0, 6.0, -0.0, -0.5, -1.0, -1.5, -2.0, -3.0, -4.0, -6.0])


def pack_weight(w, fmt):
    k, n = w.shape
    w = f64(np.asarray(w, np.float32).astype(ml_dtypes.bfloat16)).reshape(k // 32, 32, n)
    amax = np.abs(w).max(1)
    if fmt == "e4m3":
        byte = np.frexp(amax)[1] - 1 + 127 - 7
    else:
        mant, ex = np.frexp(amax / 6.0)
        byte = np.where(mant > 0.5, ex, ex - 1) + 127
    byte = np.clip(np.where(amax > 0, byte, 1), 1, 254)
    scaled = (w * np.exp2(127.0 - byte)[:, None, :]).reshape(k, n).astype(np.float32)
    by_word = np.ascontiguousarray(scaled.reshape(k // 512, 128, 4, n).transpose(0, 1, 3, 2))
    if fmt == "e4m3":
        words = by_word.astype(ml_dtypes.float8_e4m3fn).view(np.uint8)
    else:
        c = by_word.astype(ml_dtypes.float4_e2m1fn).view(np.uint8) & 0xF
        words = (c[..., 0::2] | (c[..., 1::2] << 4)).reshape(k // 512, 128, 2 * n)
    return np.ascontiguousarray(words), np.ascontiguousarray(byte.astype(np.uint8).reshape(k // 512, 16, n))


def unpack_weight(words, scales, fmt):
    g, _, n = scales.shape
    words = np.ascontiguousarray(words).reshape(g, 128, n, -1)
    if fmt == "e4m3":
        vals = words.view(ml_dtypes.float8_e4m3fn).astype(np.float64)
    else:
        nib = np.empty((g, 128, n, 4), np.uint8)
        nib[..., 0::2] = words & 0xF
        nib[..., 1::2] = words >> 4
        vals = E2M1[nib]
    vals = vals * np.repeat(np.exp2(scales.astype(np.float64) - 127.0), 8, axis=1)[..., None]
    return vals.transpose(0, 1, 3, 2).reshape(g * 512, n)


def gelu(v):
    return 0.5 * v * (1.0 + np.tanh(np.sqrt(2.0 / np.pi) * (v + 0.044715 * v**3)))


def striped8(idx):
    return np.concatenate([v.reshape(-1, 16).T for v in idx]).astype(np.uint16)


def unstriped8(offs):
    return np.stack([offs[16 * g:16 * g + 16].T.reshape(-1) for g in range(8)]).astype(np.int64)


def heads(h, wgt, idx8):
    r = np.arange(h.shape[0])
    return wgt[r // 4 % 128] * h[r[:, None], idx8[r % 512 // 64]]


K, T, S, H, P, N = 512, 4096, 2048, 1024, 1024, 768

def setup_inputs():
    n = np.random.standard_normal
    s = mx_kscale(K)[:, None]
    u = mx_kscale(H)[:, None]
    tab_words, tab_scales = pack_weight(n((K, T)) * s, "e4m3")
    w1 = n((K, H)) / np.sqrt(K) / s
    gain = 0.9 * np.exp(0.4 * n(H)) * u[:, 0]
    w4_words, w4_scales = pack_weight(1.8 * n((H, N)) / np.sqrt(H) / u, "e2m1")
    return {
        "tab_words": tab_words, "tab_scales": tab_scales,
        "offs": striped(np.random.permutation(T)[:S]),
        "w1": w1.astype(np.float32),
        "gain": gain.astype(np.float32),
        "offs2": striped8(np.stack([np.random.permutation(S)[:P] for _ in range(8)])),
        "offs3": striped8(np.stack([np.random.permutation(S)[:P] for _ in range(8)])),
        "wga": np.repeat(np.random.uniform(0.5, 2.0, (8, P)), 16, axis=0).astype(np.float32),
        "wgb": np.repeat(np.random.uniform(0.5, 2.0, (8, P)), 16, axis=0).astype(np.float32),
        "w4_words": w4_words, "w4_scales": w4_scales,
        "rain": (0.8 * n((N, P))).astype(np.float32),
    }

def reference(tab_words, tab_scales, offs, w1, gain, offs2, offs3, wga, wgb, w4_words, w4_scales, rain):
    v = unpack_weight(tab_words, tab_scales, "e4m3")[:, unstriped(offs)]
    d = mxq(f64(w1), 0, "e4m3").T @ v
    h = f64(gain)[:, None] * np.square(d)
    xa = heads(h, f64(wga), unstriped8(offs2))
    xb = heads(h, f64(wgb), unstriped8(offs3))
    x = np.minimum(xa, xb)
    w4 = unpack_weight(w4_words, w4_scales, "e2m1")
    y = w4.T @ mxq(x, 0, "e4m3")
    return y * np.tanh(y + f64(rain))

@@ -1,0 +1,267 @@
+from contextlib import ExitStack
+
+import concourse.mybir as mybir
+from concourse.masks import make_identity
+
+K, T, S, H, M, N = 512, 4096, 2048, 1024, 1024, 768
+FLOPS = 2 * K * H * S + 2 * H * N * M
+
+F32 = mybir.dt.float32
+BF16 = mybir.dt.bfloat16
+I32 = mybir.dt.int32
+U32 = mybir.dt.uint32
+U16 = mybir.dt.uint16
+U8 = mybir.dt.uint8
+FP8X4 = mybir.dt.float8_e4m3fn_x4
+FP4X4 = mybir.dt.float4_e2m1fn_x4
+ALU = mybir.AluOpType
+ACT = mybir.ActivationFunctionType
+
+P = 128
+PACK = 4
+BANK = 512
+PASSES = H // (P * PACK)
+SLICES = PASSES * PACK
+N_TILES = N // P
+S_CHUNKS = S // BANK
+M_CHUNKS = M // BANK
+H_BANKS = 4
+CHUNKS = ((0, 512), (512, 512))
+
+
+def tile_list_lichen_pollution_scores_kernel(
+    tc, tab_words, tab_scales, offs, w1, gain, offs2, offs3, wga, wgb, w4_words, w4_scales, rain, out
+):
+    nc = tc.nc
+    with ExitStack() as ctx:
+        keep = ctx.enter_context(tc.tile_pool(name="keep", bufs=1))
+        ring = ctx.enter_context(tc.tile_pool(name="ring", bufs=2))
+        psum = ctx.enter_context(tc.psum_pool(name="psum", bufs=1))
+
+        def bank(number, shape):
+            return psum.tile(shape, F32, name="bank%d" % number, tag="bank%d" % number)
+
+        list1 = keep.tile([P, S // 16], U16)
+        list2 = keep.tile([P, M // 16], U16)
+        list3 = keep.tile([P, M // 16], U16)
+        table_scales = keep.tile([P, T], U8, align_bytes=64)
+        table_words = keep.tile([P, T], I32, align_bytes=64)
+        nc.sync.dma_start(list1[:], offs)
+        for q in range(4):
+            nc.sync.dma_start(
+                table_scales[32 * q : 32 * (q + 1), :].bitcast(I32),
+                tab_scales[0, 4 * q : 4 * q + 4, :].bitcast(I32).unsqueeze(0).to_broadcast([8, 4, T // 4]),
+            )
+        nc.sync.dma_start(table_words[:], tab_words[0].rearrange("p t i -> p (t i)").bitcast(I32))
+        w1_rows = w1.rearrange("(p j) r -> p j r", j=PACK)
+        w1_raw = [keep.tile([P, PACK, BANK], F32, name="w1_raw%d" % b) for b in range(PASSES)]
+        nc.sync.dma_start(w1_raw[0][:], w1_rows[:, :, 0:BANK])
+        gains = keep.tile([P, PASSES, PACK], F32)
+        nc.sync.dma_start(gains[:], gain.rearrange("(b p i) -> p b i", b=PASSES, i=PACK))
+        weight_a = keep.tile([P, M], F32)
+        weight_b = keep.tile([P, M], F32)
+        nc.sync.dma_start(list2[:], offs2)
+        nc.sync.dma_start(weight_a[:], wga)
+        nc.sync.dma_start(list3[:], offs3)
+        nc.sync.dma_start(weight_b[:], wgb)
+        nc.sync.dma_start(w1_raw[1][:], w1_rows[:, :, BANK : 2 * BANK])
+
+        w4_codes = keep.tile([P, PASSES, 2 * N], U8, align_bytes=64)
+        w4_plane = keep.tile([P, PASSES, N], U8, align_bytes=64)
+        nc.gpsimd.memset(w4_plane[:].bitcast(I32), 0)
+        nc.sync.dma_start(w4_codes[:].bitcast(I32), w4_words.rearrange("a p c -> p a c").bitcast(I32))
+        for q in range(4):
+            nc.sync.dma_start(
+                w4_plane[32 * q : 32 * q + 4, :, :].bitcast(I32),
+                w4_scales[:, 4 * q : 4 * q + 4, :].rearrange("a r c -> r a c").bitcast(I32),
+            )
+        rain_rows = rain.rearrange("(t p) m -> p t m", p=P)
+        rains = [keep.tile([P, N_TILES, BANK], F32, name="rain%d" % c) for c in range(M_CHUNKS)]
+        for c in range(M_CHUNKS):
+            nc.sync.dma_start(rains[c][:], rain_rows[:, :, c * BANK : (c + 1) * BANK])
+        identity = keep.tile([P, P], F32)
+        make_identity(nc, identity[:])
+
+        v_scales = [keep.tile([P, 2 * BANK], U8, name="v_scales%d" % u, align_bytes=64) for u in range(S_CHUNKS // 2)]
+        v_words = [keep.tile([P, BANK], U32, name="v_words%d" % c, align_bytes=64) for c in range(S_CHUNKS)]
+        for u in range(S_CHUNKS // 2):
+            nc.vector.tensor_copy(v_scales[u][:], table_scales[:].indirect(list1[:, 64 * u : 64 * (u + 1)]))
+
+        def gather_words(c):
+            nc.vector.tensor_copy(
+                v_words[c][:], table_words[:].bitcast(U32).indirect(list1[:, 32 * c : 32 * (c + 1)])
+            )
+
+        w1_codes = {}
+        w1_planes = {}
+
+        def prepare_w1(b, first, count):
+            grouped = ring.tile([P, count, P, PACK], BF16, name="w1_grouped", tag="w1_grouped", align_bytes=64)
+            nc.scalar.copy(
+                grouped[:].rearrange("p t m j -> p m j t"),
+                w1_raw[b][:].rearrange("p j (m t) -> p m j t", t=PACK)[:, :, :, first : first + count],
+            )
+            codes = keep.tile([P, count * P], U32, name="w1_codes%d_%d" % (b, first), align_bytes=64)
+            plane = keep.tile([P, count * P], U8, name="w1_plane%d_%d" % (b, first), align_bytes=64)
+            nc.vector.quantize_mx(
+                out=codes[:].bitcast(FP8X4), scales=plane[:], in_=grouped[:].rearrange("p t m j -> p (t m j)")
+            )
+            for t in range(count):
+                w1_codes[PACK * b + first + t] = codes[:, t * P : (t + 1) * P]
+                w1_planes[PACK * b + first + t] = plane[:, t * P : (t + 1) * P]
+
+        h_tiles = {}
+
+        def make_h(s):
+            b, i = divmod(s, PACK)
+            h = ring.tile([P, S], F32, name="h", tag="h", bufs=4)
+            squares = ring.tile([P, S], F32, name="squares", tag="squares")
+            for c in range(S_CHUNKS):
+                cols = slice(c * BANK, (c + 1) * BANK)
+                d = bank((s * S_CHUNKS + c) % H_BANKS, [P, BANK])
+                nc.tensor.matmul_mx(
+                    out=d[:],
+                    lhsT=w1_codes[s].bitcast(FP8X4),
+                    lhsT_scale=w1_planes[s],
+                    rhs=v_words[c][:].bitcast(FP8X4),
+                    rhs_scale=v_scales[c // 2][:, (c % 2) * BANK : (c % 2 + 1) * BANK],
+                    start=True,
+                    stop=True,
+                )
+                nc.scalar.activation(squares[:, cols], d[:], ACT.Square)
+                if s == 0:
+                    nc.vector.tensor_scalar(h[:, cols], squares[:, cols], gains[:, b, i : i + 1], None, ALU.mult)
+            if s > 0:
+                nc.scalar.activation(h[:], squares[:], ACT.Copy, scale=gains[:, b, i : i + 1])
+            h_tiles[s] = h
+
+        def new_picks(width):
+            picks_a = keep.tile([P, PACK, width], F32, name="picks_a", tag="picks_a")
+            picks_b = keep.tile([P, PACK, width], F32, name="picks_b", tag="picks_b")
+            return picks_a, picks_b
+
+        def pick(picks, s, lo, width):
+            for side, offsets, weight in zip(picks, (list2, list3), (weight_a, weight_b)):
+                nc.vector.tensor_tensor(
+                    side[:, s % PACK, :],
+                    h_tiles[s][:].indirect(offsets[:, lo // 16 : (lo + width) // 16]),
+                    weight[:, lo : lo + width],
+                    ALU.mult,
+                )
+
+        x_codes = {}
+        x_planes = {}
+
+        def smaller(picks, lo, width):
+            x = ring.tile([P, width, PACK], BF16, name="x", tag="x", align_bytes=64)
+            nc.vector.tensor_tensor(
+                x[:].rearrange("p (g j) t -> p g t j", j=4),
+                picks[0][:, :, lo : lo + width].rearrange("p t (g j) -> p g t j", j=4),
+                picks[1][:, :, lo : lo + width].rearrange("p t (g j) -> p g t j", j=4),
+                ALU.min,
+            )
+            return x
+
+        def quantise_x(b, c, x):
+            width = CHUNKS[c][1]
+            codes = keep.tile([P, width], U32, name="x_codes%d_%d" % (b, c), align_bytes=64)
+            plane = keep.tile([P, width], U8, name="x_plane%d_%d" % (b, c), align_bytes=64)
+            nc.vector.quantize_mx(out=codes[:].bitcast(FP8X4), scales=plane[:], in_=x[:].rearrange("p m t -> p (m t)"))
+            x_codes[b, c] = codes
+            x_planes[b, c] = plane
+
+        def product(tiles, c, y):
+            for e, n in enumerate(tiles):
+                for b in range(PASSES):
+                    nc.tensor.matmul_mx(
+                        out=y[:, e, :],
+                        lhsT=w4_codes[:, b, 2 * P * n : 2 * P * (n + 1)].bitcast(FP4X4),
+                        lhsT_scale=w4_plane[:, b, P * n : P * (n + 1)],
+                        rhs=x_codes[b, c][:].bitcast(FP8X4),
+                        rhs_scale=x_planes[b, c][:],
+                        start=(b == 0),
+                        stop=(b == PASSES - 1),
+                    )
+
+        out_rows = out.rearrange("(t p) m -> p t m", p=P)
+
+        def rain_of(tiles, c):
+            lo, width = CHUNKS[c]
+            return rains[lo // BANK][:, tiles[0] : tiles[-1] + 1, lo % BANK : lo % BANK + width]
+
+        def store(tiles, c, result):
+            lo, width = CHUNKS[c]
+            nc.sync.dma_start(out_rows[:, tiles[0] : tiles[-1] + 1, lo : lo + width], result[:])
+
+        blocks = BANK // P
+
+        def finish_by_transposes(tiles, c, u):
+            shape = [P, len(tiles), CHUNKS[c][1]]
+            per_tile = CHUNKS[c][1] // P
+            y = bank(u % 2, shape)
+            product(tiles, c, y)
+            y_sb = ring.tile(shape, F32, name="y_sb", tag="y_sb", bufs=6)
+            nc.scalar.copy(y_sb[:], y[:])
+            z = bank(2 + u % 2, [P, blocks, P])
+            for source, first, final in ((rain_of(tiles, c), True, False), (y_sb[:], False, True)):
+                for k in range(blocks):
+                    e, j = divmod(k, per_tile)
+                    nc.tensor.matmul(
+                        z[:, k, :], source[:, e, j * P : (j + 1) * P], identity[:],
+                        start=(first and k == 0), stop=(final and k == blocks - 1), is_transpose=True,
+                    )
+            bend_t = ring.tile([P, blocks, P], F32, name="bend_t", tag="bend_t")
+            nc.scalar.activation(bend_t[:], z[:], ACT.Tanh)
+            bend = bank(4 + u % 4, shape)
+            for k in range(blocks):
+                e, j = divmod(k, per_tile)
+                nc.tensor.transpose(bend[:, e, j * P : (j + 1) * P], bend_t[:, k, :], identity[:])
+            result = ring.tile(shape, F32, name="result", tag="result", bufs=4)
+            nc.vector.tensor_tensor(result[:], bend[:], y_sb[:], ALU.mult)
+            store(tiles, c, result)
+
+        def finish_directly(tiles, c, u):
+            shape = [P, len(tiles), CHUNKS[c][1]]
+            y = bank(u % 8, shape)
+            product(tiles, c, y)
+            z = ring.tile(shape, F32, name="z_sb", tag="z_sb", bufs=3)
+            nc.vector.tensor_tensor(z[:], y[:], rain_of(tiles, c), ALU.add)
+            bend = ring.tile(shape, F32, name="bend_sb", tag="bend_sb", bufs=3)
+            nc.scalar.activation(bend[:], z[:], ACT.Tanh)
+            result = ring.tile(shape, F32, name="result", tag="result", bufs=4)
+            nc.vector.tensor_tensor(result[:], y[:], bend[:], ALU.mult)
+            store(tiles, c, result)
+
+        for c in range(S_CHUNKS):
+            gather_words(c)
+        prepare_w1(0, 0, 1)
+        prepare_w1(0, 1, PACK - 1)
+        make_h(0)
+        make_h(1)
+        picks = new_picks(M)
+        pick(picks, 0, 0, M)
+        make_h(2)
+        pick(picks, 1, 0, M)
+        prepare_w1(1, 0, PACK)
+        make_h(3)
+        pick(picks, 2, 0, M)
+        make_h(4)
+        pick(picks, 3, 0, M)
+        for s in range(PACK + 1, SLICES):
+            make_h(s)
+        for c, (lo, width) in enumerate(CHUNKS):
+            quantise_x(0, c, smaller(picks, lo, width))
+        unit = 0
+        for c, (lo, width) in enumerate(CHUNKS):
+            picks = new_picks(width)
+            for s in range(PACK, SLICES):
+                pick(picks, s, lo, width)
+            quantise_x(1, c, smaller(picks, 0, width))
+            together = BANK // width
+            for n in range(0, N_TILES, together):
+                tiles = list(range(n, n + together))
+                if c == len(CHUNKS) - 1:
+                    finish_directly(tiles, c, n // together)
+                else:
+                    finish_by_transposes(tiles, c, unit)
+                unit = unit + 1

@@ -25,7 +25,12 @@ SLICES = PASSES * PACK
 N_TILES = N // P
 S_CHUNKS = S // BANK
 M_CHUNKS = M // BANK
-H_BANKS = 4
+H_BANKS = 3
+Y_BANK = (0, 1, 2, 0, 1, 0)
+Z_BANK = (3, 4, 5, 6, 2, 1)
+BEND_BANK = (7, 3, 4, 5, 6, 2)
+TRANSPOSED = 5
+LAST_BANK = (1, 2, 7, 3, 4, 5)
 CHUNKS = ((0, 512), (512, 512))
 
 
@@ -98,8 +103,8 @@ def tile_list_lichen_pollution_scores_kernel(
         def prepare_w1(b, first, count):
             grouped = ring.tile([P, count, P, PACK], BF16, name="w1_grouped", tag="w1_grouped", align_bytes=64)
             nc.scalar.copy(
-                grouped[:].rearrange("p t m j -> p m j t"),
-                w1_raw[b][:].rearrange("p j (m t) -> p m j t", t=PACK)[:, :, :, first : first + count],
+                grouped[:].rearrange("p (u e) m j -> p u m j e", e=2),
+                w1_raw[b][:].rearrange("p j (m u e) -> p u m j e", u=2, e=2)[:, first // 2 : (first + count) // 2],
             )
             codes = keep.tile([P, count * P], U32, name="w1_codes%d_%d" % (b, first), align_bytes=64)
             plane = keep.tile([P, count * P], U8, name="w1_plane%d_%d" % (b, first), align_bytes=64)
@@ -155,9 +160,9 @@ def tile_list_lichen_pollution_scores_kernel(
         def smaller(picks, lo, width):
             x = ring.tile([P, width, PACK], BF16, name="x", tag="x", align_bytes=64)
             nc.vector.tensor_tensor(
-                x[:].rearrange("p (g j) t -> p g t j", j=4),
-                picks[0][:, :, lo : lo + width].rearrange("p t (g j) -> p g t j", j=4),
-                picks[1][:, :, lo : lo + width].rearrange("p t (g j) -> p g t j", j=4),
+                x[:].rearrange("p (g j) t -> p g t j", j=2),
+                picks[0][:, :, lo : lo + width].rearrange("p t (g j) -> p g t j", j=2),
+                picks[1][:, :, lo : lo + width].rearrange("p t (g j) -> p g t j", j=2),
                 ALU.min,
             )
             return x
@@ -198,11 +203,11 @@ def tile_list_lichen_pollution_scores_kernel(
         def finish_by_transposes(tiles, c, u):
             shape = [P, len(tiles), CHUNKS[c][1]]
             per_tile = CHUNKS[c][1] // P
-            y = bank(u % 2, shape)
+            y = bank(Y_BANK[u], shape)
             product(tiles, c, y)
             y_sb = ring.tile(shape, F32, name="y_sb", tag="y_sb", bufs=6)
             nc.scalar.copy(y_sb[:], y[:])
-            z = bank(2 + u % 2, [P, blocks, P])
+            z = bank(Z_BANK[u], [P, blocks, P])
             for source, first, final in ((rain_of(tiles, c), True, False), (y_sb[:], False, True)):
                 for k in range(blocks):
                     e, j = divmod(k, per_tile)
@@ -212,7 +217,7 @@ def tile_list_lichen_pollution_scores_kernel(
                     )
             bend_t = ring.tile([P, blocks, P], F32, name="bend_t", tag="bend_t")
             nc.scalar.activation(bend_t[:], z[:], ACT.Tanh)
-            bend = bank(4 + u % 4, shape)
+            bend = bank(BEND_BANK[u], shape)
             for k in range(blocks):
                 e, j = divmod(k, per_tile)
                 nc.tensor.transpose(bend[:, e, j * P : (j + 1) * P], bend_t[:, k, :], identity[:])
@@ -222,7 +227,7 @@ def tile_list_lichen_pollution_scores_kernel(
 
         def finish_directly(tiles, c, u):
             shape = [P, len(tiles), CHUNKS[c][1]]
-            y = bank(u % 8, shape)
+            y = bank(u, shape)
             product(tiles, c, y)
             z = ring.tile(shape, F32, name="z_sb", tag="z_sb", bufs=3)
             nc.vector.tensor_tensor(z[:], y[:], rain_of(tiles, c), ALU.add)
@@ -234,8 +239,8 @@ def tile_list_lichen_pollution_scores_kernel(
 
         for c in range(S_CHUNKS):
             gather_words(c)
-        prepare_w1(0, 0, 1)
-        prepare_w1(0, 1, PACK - 1)
+        prepare_w1(0, 0, 2)
+        prepare_w1(0, 2, 2)
         make_h(0)
         make_h(1)
         picks = new_picks(M)
@@ -249,8 +254,9 @@ def tile_list_lichen_pollution_scores_kernel(
         pick(picks, 3, 0, M)
         for s in range(PACK + 1, SLICES):
             make_h(s)
-        for c, (lo, width) in enumerate(CHUNKS):
-            quantise_x(0, c, smaller(picks, lo, width))
+        xs = [smaller(picks, lo, width) for lo, width in CHUNKS]
+        for c, x in enumerate(xs):
+            quantise_x(0, c, x)
         unit = 0
         for c, (lo, width) in enumerate(CHUNKS):
             picks = new_picks(width)
@@ -261,7 +267,9 @@ def tile_list_lichen_pollution_scores_kernel(
             for n in range(0, N_TILES, together):
                 tiles = list(range(n, n + together))
                 if c == len(CHUNKS) - 1:
-                    finish_directly(tiles, c, n // together)
+                    finish_directly(tiles, c, LAST_BANK[n])
+                elif n >= TRANSPOSED:
+                    finish_directly(tiles, c, Y_BANK[n])
                 else:
                     finish_by_transposes(tiles, c, unit)
                 unit = unit + 1

@@ -26,11 +26,10 @@ N_TILES = N // P
 S_CHUNKS = S // BANK
 M_CHUNKS = M // BANK
 H_BANKS = 3
-Y_BANK = (0, 1, 2, 0, 1, 0)
-Z_BANK = (3, 4, 5, 6, 2, 1)
-BEND_BANK = (7, 3, 4, 5, 6, 2)
-TRANSPOSED = 5
-LAST_BANK = (1, 2, 7, 3, 4, 5)
+Y_BANK = (0, 1, 2, 0, 1, 0, 0, 7, 4, 5, 6, 2)
+Z_BANK = (3, 4, 5, 6, 2, 1, 1, 3)
+BEND_BANK = (7, 3, 4, 5, 6, 2, 0, 7)
+TRANSPOSED = 8
 CHUNKS = ((0, 512), (512, 512))
 
 
@@ -87,12 +86,12 @@ def tile_list_lichen_pollution_scores_kernel(
         identity = keep.tile([P, P], F32)
         make_identity(nc, identity[:])
 
-        v_scales = [keep.tile([P, 2 * BANK], U8, name="v_scales%d" % u, align_bytes=64) for u in range(S_CHUNKS // 2)]
-        v_words = [keep.tile([P, BANK], U32, name="v_words%d" % c, align_bytes=64) for c in range(S_CHUNKS)]
-        for u in range(S_CHUNKS // 2):
-            nc.vector.tensor_copy(v_scales[u][:], table_scales[:].indirect(list1[:, 64 * u : 64 * (u + 1)]))
+        v_scales = keep.tile([P, S], U8, align_bytes=64)
+        v_words = {}
+        nc.vector.tensor_copy(v_scales[:], table_scales[:].indirect(list1[:]))
 
-        def gather_words(c):
+        def gather_words(c, tag):
+            v_words[c] = keep.tile([P, BANK], U32, name="v_words%d" % c, tag=tag, align_bytes=64)
             nc.vector.tensor_copy(
                 v_words[c][:], table_words[:].bitcast(U32).indirect(list1[:, 32 * c : 32 * (c + 1)])
             )
@@ -100,8 +99,8 @@ def tile_list_lichen_pollution_scores_kernel(
         w1_codes = {}
         w1_planes = {}
 
-        def prepare_w1(b, first, count):
-            grouped = ring.tile([P, count, P, PACK], BF16, name="w1_grouped", tag="w1_grouped", align_bytes=64)
+        def prepare_w1(b, first, count, tag):
+            grouped = keep.tile([P, count, P, PACK], BF16, name="w1_grouped", tag=tag, align_bytes=64)
             nc.scalar.copy(
                 grouped[:].rearrange("p (u e) m j -> p u m j e", e=2),
                 w1_raw[b][:].rearrange("p j (m u e) -> p u m j e", u=2, e=2)[:, first // 2 : (first + count) // 2],
@@ -129,7 +128,7 @@ def tile_list_lichen_pollution_scores_kernel(
                     lhsT=w1_codes[s].bitcast(FP8X4),
                     lhsT_scale=w1_planes[s],
                     rhs=v_words[c][:].bitcast(FP8X4),
-                    rhs_scale=v_scales[c // 2][:, (c % 2) * BANK : (c % 2 + 1) * BANK],
+                    rhs_scale=v_scales[:, cols],
                     start=True,
                     stop=True,
                 )
@@ -169,8 +168,12 @@ def tile_list_lichen_pollution_scores_kernel(
 
         def quantise_x(b, c, x):
             width = CHUNKS[c][1]
-            codes = keep.tile([P, width], U32, name="x_codes%d_%d" % (b, c), align_bytes=64)
-            plane = keep.tile([P, width], U8, name="x_plane%d_%d" % (b, c), align_bytes=64)
+            if (b, c) == (PASSES - 1, len(CHUNKS) - 1):
+                codes = ring.tile([P, width], U32, name="x_codes_last", tag="bend_t0", align_bytes=64)
+                plane = ring.tile([P, width], U8, name="x_plane_last", tag="bend_t0", align_bytes=64)
+            else:
+                codes = keep.tile([P, width], U32, name="x_codes%d_%d" % (b, c), align_bytes=64)
+                plane = keep.tile([P, width], U8, name="x_plane%d_%d" % (b, c), align_bytes=64)
             nc.vector.quantize_mx(out=codes[:].bitcast(FP8X4), scales=plane[:], in_=x[:].rearrange("p m t -> p (m t)"))
             x_codes[b, c] = codes
             x_planes[b, c] = plane
@@ -215,13 +218,13 @@ def tile_list_lichen_pollution_scores_kernel(
                         z[:, k, :], source[:, e, j * P : (j + 1) * P], identity[:],
                         start=(first and k == 0), stop=(final and k == blocks - 1), is_transpose=True,
                     )
-            bend_t = ring.tile([P, blocks, P], F32, name="bend_t", tag="bend_t")
+            bend_t = ring.tile([P, blocks, P], F32, name="bend_t", tag="bend_t%d" % c, align_bytes=64)
             nc.scalar.activation(bend_t[:], z[:], ACT.Tanh)
             bend = bank(BEND_BANK[u], shape)
             for k in range(blocks):
                 e, j = divmod(k, per_tile)
                 nc.tensor.transpose(bend[:, e, j * P : (j + 1) * P], bend_t[:, k, :], identity[:])
-            result = ring.tile(shape, F32, name="result", tag="result", bufs=4)
+            result = ring.tile(shape, F32, name="result", tag="result", bufs=6)
             nc.vector.tensor_tensor(result[:], bend[:], y_sb[:], ALU.mult)
             store(tiles, c, result)
 
@@ -229,25 +232,26 @@ def tile_list_lichen_pollution_scores_kernel(
             shape = [P, len(tiles), CHUNKS[c][1]]
             y = bank(u, shape)
             product(tiles, c, y)
-            z = ring.tile(shape, F32, name="z_sb", tag="z_sb", bufs=3)
+            z = ring.tile(shape, F32, name="z_sb", tag="z_sb", bufs=4)
             nc.vector.tensor_tensor(z[:], y[:], rain_of(tiles, c), ALU.add)
-            bend = ring.tile(shape, F32, name="bend_sb", tag="bend_sb", bufs=3)
+            bend = ring.tile(shape, F32, name="bend_sb", tag="bend_sb", bufs=4)
             nc.scalar.activation(bend[:], z[:], ACT.Tanh)
-            result = ring.tile(shape, F32, name="result", tag="result", bufs=4)
+            result = ring.tile(shape, F32, name="result", tag="result", bufs=6)
             nc.vector.tensor_tensor(result[:], y[:], bend[:], ALU.mult)
             store(tiles, c, result)
 
-        for c in range(S_CHUNKS):
-            gather_words(c)
-        prepare_w1(0, 0, 2)
-        prepare_w1(0, 2, 2)
+        for c in range(S_CHUNKS - 1):
+            gather_words(c, "v_words%d" % c)
+        prepare_w1(0, 0, 2, "first_pair")
+        gather_words(S_CHUNKS - 1, "first_pair")
+        prepare_w1(0, 2, 2, "w1_grouped")
         make_h(0)
         make_h(1)
         picks = new_picks(M)
         pick(picks, 0, 0, M)
         make_h(2)
         pick(picks, 1, 0, M)
-        prepare_w1(1, 0, PACK)
+        prepare_w1(1, 0, PACK, "w1_grouped")
         make_h(3)
         pick(picks, 2, 0, M)
         make_h(4)
@@ -266,10 +270,8 @@ def tile_list_lichen_pollution_scores_kernel(
             together = BANK // width
             for n in range(0, N_TILES, together):
                 tiles = list(range(n, n + together))
-                if c == len(CHUNKS) - 1:
-                    finish_directly(tiles, c, LAST_BANK[n])
-                elif n >= TRANSPOSED:
-                    finish_directly(tiles, c, Y_BANK[n])
-                else:
+                if unit < TRANSPOSED:
                     finish_by_transposes(tiles, c, unit)
+                else:
+                    finish_directly(tiles, c, Y_BANK[unit])
                 unit = unit + 1

from contextlib import ExitStack

import concourse.mybir as mybir
from concourse.masks import make_identity

K, T, S, H, M, N = 512, 4096, 2048, 1024, 1024, 768
FLOPS = 2 * K * H * S + 2 * H * N * M

F32 = mybir.dt.float32
BF16 = mybir.dt.bfloat16
I32 = mybir.dt.int32
U32 = mybir.dt.uint32
U16 = mybir.dt.uint16
U8 = mybir.dt.uint8
FP8X4 = mybir.dt.float8_e4m3fn_x4
FP4X4 = mybir.dt.float4_e2m1fn_x4
ALU = mybir.AluOpType
ACT = mybir.ActivationFunctionType

P = 128
PACK = 4
BANK = 512
PASSES = H // (P * PACK)
SLICES = PASSES * PACK
N_TILES = N // P
S_CHUNKS = S // BANK
M_CHUNKS = M // BANK
H_BANKS = 3
Y_BANK = (0, 1, 2, 0, 1, 0, 0, 7, 4, 5, 6, 2)
Z_BANK = (3, 4, 5, 6, 2, 1, 1, 3)
BEND_BANK = (7, 3, 4, 5, 6, 2, 0, 7)
TRANSPOSED = 8
CHUNKS = ((0, 512), (512, 512))


def tile_list_lichen_pollution_scores_kernel(
    tc, tab_words, tab_scales, offs, w1, gain, offs2, offs3, wga, wgb, w4_words, w4_scales, rain, out
):
    nc = tc.nc
    with ExitStack() as ctx:
        keep = ctx.enter_context(tc.tile_pool(name="keep", bufs=1))
        ring = ctx.enter_context(tc.tile_pool(name="ring", bufs=2))
        psum = ctx.enter_context(tc.psum_pool(name="psum", bufs=1))

        def bank(number, shape):
            return psum.tile(shape, F32, name="bank%d" % number, tag="bank%d" % number)

        list1 = keep.tile([P, S // 16], U16)
        list2 = keep.tile([P, M // 16], U16)
        list3 = keep.tile([P, M // 16], U16)
        table_scales = keep.tile([P, T], U8, align_bytes=64)
        table_words = keep.tile([P, T], I32, align_bytes=64)
        nc.sync.dma_start(list1[:], offs)
        for q in range(4):
            nc.sync.dma_start(
                table_scales[32 * q : 32 * (q + 1), :].bitcast(I32),
                tab_scales[0, 4 * q : 4 * q + 4, :].bitcast(I32).unsqueeze(0).to_broadcast([8, 4, T // 4]),
            )
        nc.sync.dma_start(table_words[:], tab_words[0].rearrange("p t i -> p (t i)").bitcast(I32))
        w1_rows = w1.rearrange("(p j) r -> p j r", j=PACK)
        w1_raw = [keep.tile([P, PACK, BANK], F32, name="w1_raw%d" % b) for b in range(PASSES)]
        nc.sync.dma_start(w1_raw[0][:], w1_rows[:, :, 0:BANK])
        gains = keep.tile([P, PASSES, PACK], F32)
        nc.sync.dma_start(gains[:], gain.rearrange("(b p i) -> p b i", b=PASSES, i=PACK))
        weight_a = keep.tile([P, M], F32)
        weight_b = keep.tile([P, M], F32)
        nc.sync.dma_start(list2[:], offs2)
        nc.sync.dma_start(weight_a[:], wga)
        nc.sync.dma_start(list3[:], offs3)
        nc.sync.dma_start(weight_b[:], wgb)
        nc.sync.dma_start(w1_raw[1][:], w1_rows[:, :, BANK : 2 * BANK])

        w4_codes = keep.tile([P, PASSES, 2 * N], U8, align_bytes=64)
        w4_plane = keep.tile([P, PASSES, N], U8, align_bytes=64)
        nc.gpsimd.memset(w4_plane[:].bitcast(I32), 0)
        nc.sync.dma_start(w4_codes[:].bitcast(I32), w4_words.rearrange("a p c -> p a c").bitcast(I32))
        for q in range(4):
            nc.sync.dma_start(
                w4_plane[32 * q : 32 * q + 4, :, :].bitcast(I32),
                w4_scales[:, 4 * q : 4 * q + 4, :].rearrange("a r c -> r a c").bitcast(I32),
            )
        rain_rows = rain.rearrange("(t p) m -> p t m", p=P)
        rains = [keep.tile([P, N_TILES, BANK], F32, name="rain%d" % c) for c in range(M_CHUNKS)]
        for c in range(M_CHUNKS):
            nc.sync.dma_start(rains[c][:], rain_rows[:, :, c * BANK : (c + 1) * BANK])
        identity = keep.tile([P, P], F32)
        make_identity(nc, identity[:])

        v_scales = keep.tile([P, S], U8, align_bytes=64)
        v_words = {}
        nc.vector.tensor_copy(v_scales[:], table_scales[:].indirect(list1[:]))

        def gather_words(c, tag):
            v_words[c] = keep.tile([P, BANK], U32, name="v_words%d" % c, tag=tag, align_bytes=64)
            nc.vector.tensor_copy(
                v_words[c][:], table_words[:].bitcast(U32).indirect(list1[:, 32 * c : 32 * (c + 1)])
            )

        w1_codes = {}
        w1_planes = {}

        def prepare_w1(b, first, count, tag):
            grouped = keep.tile([P, count, P, PACK], BF16, name="w1_grouped", tag=tag, align_bytes=64)
            nc.scalar.copy(
                grouped[:].rearrange("p (u e) m j -> p u m j e", e=2),
                w1_raw[b][:].rearrange("p j (m u e) -> p u m j e", u=2, e=2)[:, first // 2 : (first + count) // 2],
            )
            codes = keep.tile([P, count * P], U32, name="w1_codes%d_%d" % (b, first), align_bytes=64)
            plane = keep.tile([P, count * P], U8, name="w1_plane%d_%d" % (b, first), align_bytes=64)
            nc.vector.quantize_mx(
                out=codes[:].bitcast(FP8X4), scales=plane[:], in_=grouped[:].rearrange("p t m j -> p (t m j)")
            )
            for t in range(count):
                w1_codes[PACK * b + first + t] = codes[:, t * P : (t + 1) * P]
                w1_planes[PACK * b + first + t] = plane[:, t * P : (t + 1) * P]

        h_tiles = {}

        def make_h(s):
            b, i = divmod(s, PACK)
            h = ring.tile([P, S], F32, name="h", tag="h", bufs=4)
            squares = ring.tile([P, S], F32, name="squares", tag="squares")
            for c in range(S_CHUNKS):
                cols = slice(c * BANK, (c + 1) * BANK)
                d = bank((s * S_CHUNKS + c) % H_BANKS, [P, BANK])
                nc.tensor.matmul_mx(
                    out=d[:],
                    lhsT=w1_codes[s].bitcast(FP8X4),
                    lhsT_scale=w1_planes[s],
                    rhs=v_words[c][:].bitcast(FP8X4),
                    rhs_scale=v_scales[:, cols],
                    start=True,
                    stop=True,
                )
                nc.scalar.activation(squares[:, cols], d[:], ACT.Square)
                if s == 0:
                    nc.vector.tensor_scalar(h[:, cols], squares[:, cols], gains[:, b, i : i + 1], None, ALU.mult)
            if s > 0:
                nc.scalar.activation(h[:], squares[:], ACT.Copy, scale=gains[:, b, i : i + 1])
            h_tiles[s] = h

        def new_picks(width):
            picks_a = keep.tile([P, PACK, width], F32, name="picks_a", tag="picks_a")
            picks_b = keep.tile([P, PACK, width], F32, name="picks_b", tag="picks_b")
            return picks_a, picks_b

        def pick(picks, s, lo, width):
            for side, offsets, weight in zip(picks, (list2, list3), (weight_a, weight_b)):
                nc.vector.tensor_tensor(
                    side[:, s % PACK, :],
                    h_tiles[s][:].indirect(offsets[:, lo // 16 : (lo + width) // 16]),
                    weight[:, lo : lo + width],
                    ALU.mult,
                )

        x_codes = {}
        x_planes = {}

        def smaller(picks, lo, width):
            x = ring.tile([P, width, PACK], BF16, name="x", tag="x", align_bytes=64)
            nc.vector.tensor_tensor(
                x[:].rearrange("p (g j) t -> p g t j", j=2),
                picks[0][:, :, lo : lo + width].rearrange("p t (g j) -> p g t j", j=2),
                picks[1][:, :, lo : lo + width].rearrange("p t (g j) -> p g t j", j=2),
                ALU.min,
            )
            return x

        def quantise_x(b, c, x):
            width = CHUNKS[c][1]
            if (b, c) == (PASSES - 1, len(CHUNKS) - 1):
                codes = ring.tile([P, width], U32, name="x_codes_last", tag="bend_t0", align_bytes=64)
                plane = ring.tile([P, width], U8, name="x_plane_last", tag="bend_t0", align_bytes=64)
            else:
                codes = keep.tile([P, width], U32, name="x_codes%d_%d" % (b, c), align_bytes=64)
                plane = keep.tile([P, width], U8, name="x_plane%d_%d" % (b, c), align_bytes=64)
            nc.vector.quantize_mx(out=codes[:].bitcast(FP8X4), scales=plane[:], in_=x[:].rearrange("p m t -> p (m t)"))
            x_codes[b, c] = codes
            x_planes[b, c] = plane

        def product(tiles, c, y):
            for e, n in enumerate(tiles):
                for b in range(PASSES):
                    nc.tensor.matmul_mx(
                        out=y[:, e, :],
                        lhsT=w4_codes[:, b, 2 * P * n : 2 * P * (n + 1)].bitcast(FP4X4),
                        lhsT_scale=w4_plane[:, b, P * n : P * (n + 1)],
                        rhs=x_codes[b, c][:].bitcast(FP8X4),
                        rhs_scale=x_planes[b, c][:],
                        start=(b == 0),
                        stop=(b == PASSES - 1),
                    )

        out_rows = out.rearrange("(t p) m -> p t m", p=P)

        def rain_of(tiles, c):
            lo, width = CHUNKS[c]
            return rains[lo // BANK][:, tiles[0] : tiles[-1] + 1, lo % BANK : lo % BANK + width]

        def store(tiles, c, result):
            lo, width = CHUNKS[c]
            nc.sync.dma_start(out_rows[:, tiles[0] : tiles[-1] + 1, lo : lo + width], result[:])

        blocks = BANK // P

        def finish_by_transposes(tiles, c, u):
            shape = [P, len(tiles), CHUNKS[c][1]]
            per_tile = CHUNKS[c][1] // P
            y = bank(Y_BANK[u], shape)
            product(tiles, c, y)
            y_sb = ring.tile(shape, F32, name="y_sb", tag="y_sb", bufs=6)
            nc.scalar.copy(y_sb[:], y[:])
            z = bank(Z_BANK[u], [P, blocks, P])
            for source, first, final in ((rain_of(tiles, c), True, False), (y_sb[:], False, True)):
                for k in range(blocks):
                    e, j = divmod(k, per_tile)
                    nc.tensor.matmul(
                        z[:, k, :], source[:, e, j * P : (j + 1) * P], identity[:],
                        start=(first and k == 0), stop=(final and k == blocks - 1), is_transpose=True,
                    )
            bend_t = ring.tile([P, blocks, P], F32, name="bend_t", tag="bend_t%d" % c, align_bytes=64)
            nc.scalar.activation(bend_t[:], z[:], ACT.Tanh)
            bend = bank(BEND_BANK[u], shape)
            for k in range(blocks):
                e, j = divmod(k, per_tile)
                nc.tensor.transpose(bend[:, e, j * P : (j + 1) * P], bend_t[:, k, :], identity[:])
            result = ring.tile(shape, F32, name="result", tag="result", bufs=6)
            nc.vector.tensor_tensor(result[:], bend[:], y_sb[:], ALU.mult)
            store(tiles, c, result)

        def finish_directly(tiles, c, u):
            shape = [P, len(tiles), CHUNKS[c][1]]
            y = bank(u, shape)
            product(tiles, c, y)
            z = ring.tile(shape, F32, name="z_sb", tag="z_sb", bufs=4)
            nc.vector.tensor_tensor(z[:], y[:], rain_of(tiles, c), ALU.add)
            bend = ring.tile(shape, F32, name="bend_sb", tag="bend_sb", bufs=4)
            nc.scalar.activation(bend[:], z[:], ACT.Tanh)
            result = ring.tile(shape, F32, name="result", tag="result", bufs=6)
            nc.vector.tensor_tensor(result[:], y[:], bend[:], ALU.mult)
            store(tiles, c, result)

        for c in range(S_CHUNKS - 1):
            gather_words(c, "v_words%d" % c)
        prepare_w1(0, 0, 2, "first_pair")
        gather_words(S_CHUNKS - 1, "first_pair")
        prepare_w1(0, 2, 2, "w1_grouped")
        make_h(0)
        make_h(1)
        picks = new_picks(M)
        pick(picks, 0, 0, M)
        make_h(2)
        pick(picks, 1, 0, M)
        prepare_w1(1, 0, PACK, "w1_grouped")
        make_h(3)
        pick(picks, 2, 0, M)
        make_h(4)
        pick(picks, 3, 0, M)
        for s in range(PACK + 1, SLICES):
            make_h(s)
        xs = [smaller(picks, lo, width) for lo, width in CHUNKS]
        for c, x in enumerate(xs):
            quantise_x(0, c, x)
        unit = 0
        for c, (lo, width) in enumerate(CHUNKS):
            picks = new_picks(width)
            for s in range(PACK, SLICES):
                pick(picks, s, lo, width)
            quantise_x(1, c, smaller(picks, 0, width))
            together = BANK // width
            for n in range(0, N_TILES, together):
                tiles = list(range(n, n + together))
                if unit < TRANSPOSED:
                    finish_by_transposes(tiles, c, unit)
                else:
                    finish_directly(tiles, c, Y_BANK[unit])
                unit = unit + 1
